import numpy as np
import ml_dtypes


def mxq(x, axis, fmt="e4m3"):
    dtype, down = {"e4m3": (ml_dtypes.float8_e4m3fn, 7), "e5m2": (ml_dtypes.float8_e5m2, 14)}[fmt]
    v = np.moveaxis(np.asarray(x, np.float32).astype(ml_dtypes.bfloat16).astype(np.float64), axis, -1)
    blocks = v.reshape(v.shape[:-1] + (-1, 32))
    amax = np.abs(blocks).max(-1, keepdims=True)
    byte = np.maximum(np.where(amax > 0, np.frexp(amax)[1] - 1 + 127, 0) - down, 1)
    scale = np.exp2(byte - 127.0)
    codes = (blocks / scale).astype(np.float32).astype(dtype).astype(np.float64)
    return np.moveaxis((codes * scale).reshape(v.shape), -1, axis)


WIDE = False


def mx_kscale(k):
    if not WIDE:
        return np.ones(k)
    levels = np.array([10, -10, 5, -5, 0])
    if k % 512:
        return np.exp2(np.random.permutation(np.resize(levels, k // 32))).repeat(32)
    a = np.empty((k // 512, 16))
    for p in range(k // 512):
        a[p, :8] = np.random.permutation(np.resize(levels, 8))
        for g in range(8):
            far = levels[np.abs(levels - a[p, g]) >= 10]
            a[p, g + 8] = far[np.random.randint(len(far))]
    return np.exp2(a.ravel()).repeat(32)


def f64(x):
    return np.asarray(x).astype(np.float64)


def striped(idx):
    return np.tile(idx.reshape(-1, 16).T, (8, 1)).astype(np.uint16)


def unstriped(offs):
    return offs[:16].T.reshape(-1).astype(np.int64)


E2M1 = np.array([0.0, 0.5, 1.0, 1.5, 2.0, 3.0, 4.0, 6.0, -0.0, -0.5, -1.0, -1.5, -2.0, -3.0, -4.0, -6.0])


def pack_weight(w, fmt):
    k, n = w.shape
    w = f64(np.asarray(w, np.float32).astype(ml_dtypes.bfloat16)).reshape(k // 32, 32, n)
    amax = np.abs(w).max(1)
    if fmt == "e4m3":
        byte = np.frexp(amax)[1] - 1 + 127 - 7
    else:
        mant, ex = np.frexp(amax / 6.0)
        byte = np.where(mant > 0.5, ex, ex - 1) + 127
    byte = np.clip(np.where(amax > 0, byte, 1), 1, 254)
    scaled = (w * np.exp2(127.0 - byte)[:, None, :]).reshape(k, n).astype(np.float32)
    by_word = np.ascontiguousarray(scaled.reshape(k // 512, 128, 4, n).transpose(0, 1, 3, 2))
    if fmt == "e4m3":
        words = by_word.astype(ml_dtypes.float8_e4m3fn).view(np.uint8)
    else:
        c = by_word.astype(ml_dtypes.float4_e2m1fn).view(np.uint8) & 0xF
        words = (c[..., 0::2] | (c[..., 1::2] << 4)).reshape(k // 512, 128, 2 * n)
    return np.ascontiguousarray(words), np.ascontiguousarray(byte.astype(np.uint8).reshape(k // 512, 16, n))


def unpack_weight(words, scales, fmt):
    g, _, n = scales.shape
    words = np.ascontiguousarray(words).reshape(g, 128, n, -1)
    if fmt == "e4m3":
        vals = words.view(ml_dtypes.float8_e4m3fn).astype(np.float64)
    else:
        nib = np.empty((g, 128, n, 4), np.uint8)
        nib[..., 0::2] = words & 0xF
        nib[..., 1::2] = words >> 4
        vals = E2M1[nib]
    vals = vals * np.repeat(np.exp2(scales.astype(np.float64) - 127.0), 8, axis=1)[..., None]
    return vals.transpose(0, 1, 3, 2).reshape(g * 512, n)


def relu(v):
    return np.maximum(v, 0.0)


K, T, E, C, N = 2048, 512, 8, 256, 128
TOP = 4


def by_expert(wq, xq):
    return np.concatenate([wq[e].T @ xq[:, e * C:(e + 1) * C] for e in range(E)], axis=1)


def setup_inputs():
    n = np.random.standard_normal
    s = mx_kscale(K)[:, None]
    deal = np.repeat(np.arange(E), C).reshape(TOP, T)[:, np.random.permutation(T)]
    deal = np.take_along_axis(deal, np.argsort(np.random.rand(TOP, T), axis=0), axis=0)
    for _ in range(8):
        s_, t_ = np.random.permutation(T).reshape(2, -1); r = np.random.randint(TOP, size=T // 2); x, y = deal[r, s_].copy(), deal[r, t_].copy()
        ok = ~((deal[:, s_] == y).any(0) | (deal[:, t_] == x).any(0)); deal[r[ok], s_[ok]] = y[ok]; deal[r[ok], t_[ok]] = x[ok]
    order = np.lexsort((np.random.rand(TOP * T), deal.reshape(-1)))
    slot_token = order % T; pos = np.empty(TOP * T, np.int64); pos[order] = np.arange(TOP * T); pos = pos.reshape(TOP, T)
    g = np.random.uniform(0.5, 1.5, (TOP, T)); g = g / g.sum(0)
    w = [pack_weight(m, "e2m1") for m in n((E + 1, K, N)) / np.sqrt(K) / s[None]]
    return {
        "xT": (n((K, T)) * s).astype(np.float32),
        "w_words": np.stack([m[0] for m in w]),
        "w_scales": np.stack([m[1] for m in w]),
        "b": (0.3 * n((N, E + 1))).astype(np.float32),
        "gate": np.stack([np.tile(r, (N, 1)) for r in g]).astype(np.float32),
        "offs": striped(slot_token),
        "pos1": striped(pos[0]),
        "pos2": striped(pos[1]),
        "pos3": striped(pos[2]),
        "pos4": striped(pos[3]),
    }


def reference(xT, w_words, w_scales, b, gate, offs, pos1, pos2, pos3, pos4):
    idx = unstriped(offs)
    w = np.stack([unpack_weight(w_words[e], w_scales[e], "e2m1") for e in range(E + 1)])
    wq = w
    xs = mxq(f64(xT), 0, "e4m3")
    ys = relu((wq[E].T @ xs) + f64(b)[:, E:])
    xq = mxq(f64(xT)[:, idx], 0, "e4m3")
    y = by_expert(w, xq)
    y = relu(y + np.repeat(f64(b)[:, :E], C, axis=1))
    return ys + sum(f64(gate[r]) * y[:, unstriped(p)] for r, p in enumerate((pos1, pos2, pos3, pos4)))

@@ -1,0 +1,166 @@
+from contextlib import ExitStack
+
+import concourse.mybir as mybir
+
+K, T, E, C, N = 2048, 512, 8, 256, 128
+TOP = 4
+SLOTS = E * C
+FLOPS = 2 * K * N * (SLOTS + T)
+
+F32 = mybir.dt.float32
+BF16 = mybir.dt.bfloat16
+I32 = mybir.dt.int32
+U32 = mybir.dt.uint32
+U16 = mybir.dt.uint16
+U8 = mybir.dt.uint8
+FP8X4 = mybir.dt.float8_e4m3fn_x4
+FP4X4 = mybir.dt.float4_e2m1fn_x4
+ACT = mybir.ActivationFunctionType
+ALU = mybir.AluOpType
+
+P = 128
+PASSES = K // (4 * P)
+PLANES = 2 * PASSES
+GROUP = 128
+SPARE = 1024
+WINDOW = T + SPARE
+HALF = T // 2
+
+
+def tile_moe_shr_lin_relu_kernel(
+    tc, xT, w_words, w_scales, b, gate, offs, pos1, pos2, pos3, pos4, out
+):
+    nc = tc.nc
+    with ExitStack() as ctx:
+        keep = ctx.enter_context(tc.tile_pool(name="keep", bufs=1))
+        ring = ctx.enter_context(tc.tile_pool(name="ring", bufs=3))
+        banks = ctx.enter_context(tc.psum_pool(name="banks", bufs=6))
+        shared_bank = ctx.enter_context(tc.psum_pool(name="shared_bank", bufs=1))
+
+        x_rows = xT.rearrange("(a p u j) t -> a u p j t", a=PASSES, p=P, u=2, j=2)
+        raw = []
+        slot_tokens = keep.tile([P, SLOTS // 16], U16, name="slot_tokens")
+        for i in range(PLANES):
+            tile = keep.tile([P, 2, T], F32, name=f"raw{i}")
+            nc.sync.dma_start(tile[:], x_rows[i // 2, 1 - i % 2])
+            raw.append(tile)
+            if i == 0:
+                nc.sync.dma_start(slot_tokens[:], offs)
+
+        pairs = keep.tile([P, PLANES * T + SPARE], U32, name="pairs", align_bytes=64)
+        nc.vector.memset(pairs[:, PLANES * T :], 0)
+        w_scale = keep.tile([P, (E + 1) * PASSES, N], U8, name="w_scale", align_bytes=64)
+        nc.gpsimd.memset(w_scale[:].bitcast(I32), 0)
+        w_code = keep.tile([P, (E + 1) * PASSES, 2 * N], U8, name="w_code", align_bytes=64)
+        nc.sync.dma_start(w_code[:].bitcast(I32), w_words.rearrange("e a p c -> p (e a) c").bitcast(I32))
+        scale_rows = w_scales.rearrange("e a (q r) n -> r q (e a) n", r=4)
+        for r in range(4):
+            nc.sync.dma_start(w_scale[r:P:32, :, :].bitcast(I32), scale_rows[r].bitcast(I32))
+        bias = keep.tile([P, E + 1], F32, name="bias")
+        nc.sync.dma_start(bias[:], b)
+        gates = keep.tile([P, TOP, T], F32, name="gates")
+        nc.sync.dma_start(gates[:], gate.rearrange("r p t -> p r t"))
+        token_slots = []
+        for r, pos in enumerate((pos1, pos2, pos3, pos4)):
+            tile = keep.tile([P, T // 16], U16, name=f"token_slots{r}")
+            nc.sync.dma_start(tile[:], pos)
+            token_slots.append(tile)
+
+        def plane_start(i):
+            return (PLANES - 1 - i) * T
+
+        def cast_plane(i):
+            dst = pairs[:, plane_start(i) : plane_start(i) + T].bitcast(BF16).rearrange("p (t j) -> p t j", j=2)
+            src = raw[i][:].rearrange("p j t -> p t j")
+            if i == 0:
+                nc.vector.tensor_copy(dst, src)
+            else:
+                nc.scalar.activation(dst, src, ACT.Copy)
+
+        for i in range(PLANES):
+            cast_plane(i)
+
+        shared_words = []
+        for a in range(PASSES):
+            tile = keep.tile([P, T, 2], U32, name=f"shared_words{a}", align_bytes=64)
+            lo = plane_start(2 * a + 1)
+            both = pairs[:, lo : lo + 2 * T].rearrange("p (u t) -> p t u", u=2)
+            shared_words.append((tile, both))
+
+        y = keep.tile([P, SLOTS], F32, name="y")
+        ys = keep.tile([P, T], F32, name="ys")
+
+        chunks = []
+        for a in range(PASSES - 1):
+            chunks += [(a, 0, 1024), (a, 1024, 1024)]
+        chunks += [(3, 0, 512), (3, 512, 512), (3, 1024, 512), (3, 1536, 256), (3, 1792, 256)]
+
+        made = {}
+
+        def multiply(acc, e, a, codes, scales):
+            nc.tensor.matmul_mx(
+                out=acc,
+                lhsT=w_code[:, e * PASSES + a, :].bitcast(FP4X4),
+                lhsT_scale=w_scale[:, e * PASSES + a, :],
+                rhs=codes.bitcast(FP8X4),
+                rhs_scale=scales,
+                start=(a == 0),
+                stop=(a == PASSES - 1),
+            )
+
+        for number, (a, s0, n) in enumerate(chunks):
+            picked = ring.tile([P, 2, n], U32, name="picked", tag="picked", align_bytes=64)
+            for v in range(2):
+                i = 2 * a + v
+                window = pairs[:, plane_start(i) : plane_start(i) + WINDOW]
+                nc.vector.tensor_copy(picked[:, 1 - v, :], window.indirect(slot_tokens[:, s0 // 16 : (s0 + n) // 16]))
+            words = ring.tile([P, n, 2], U32, name="words", tag="words", align_bytes=64)
+            nc.scalar.copy(words[:], picked[:].rearrange("p u s -> p s u"))
+            codes = keep.tile([P, n], U32, name=f"codes{number}", align_bytes=64)
+            scales = keep.tile([P, n], U8, name=f"scales{number}", align_bytes=64)
+            nc.vector.quantize_mx(
+                out=codes[:].bitcast(FP8X4),
+                scales=scales[:],
+                in_=words[:].rearrange("p s u -> p (s u)").bitcast(BF16),
+            )
+            for slot in range(s0, s0 + n, GROUP):
+                cols = slice(slot - s0, slot - s0 + GROUP)
+                made[(a, slot)] = (codes[:, cols], scales[:, cols])
+            if s0 == 0:
+                tile, both = shared_words[a]
+                nc.scalar.copy(tile[:], both)
+            if a == PASSES - 1:
+                for slot in range(s0, s0 + n, GROUP):
+                    e = slot // C
+                    acc = banks.tile([P, GROUP], F32, name="acc")
+                    for a2 in range(PASSES):
+                        multiply(acc[:], e, a2, *made[(a2, slot)])
+                    nc.scalar.activation(y[:, slot : slot + GROUP], acc[:], ACT.Relu, bias=bias[:, e : e + 1])
+
+        acc = shared_bank.tile([P, T], F32, name="shared_acc")
+        for a in range(PASSES):
+            codes = ring.tile([P, T], U32, name="shared_codes", tag="picked", align_bytes=64)
+            scales = keep.tile([P, T], U8, name=f"shared_scales{a}", align_bytes=64)
+            nc.vector.quantize_mx(
+                out=codes[:].bitcast(FP8X4),
+                scales=scales[:],
+                in_=shared_words[a][0][:].rearrange("p s u -> p (s u)").bitcast(BF16),
+            )
+            multiply(acc[:], E, a, codes[:], scales[:])
+        nc.scalar.activation(ys[:], acc[:], ACT.Relu, bias=bias[:, E : E + 1])
+
+        for h in range(2):
+            cols = slice(h * HALF, (h + 1) * HALF)
+            z = keep.tile([P, TOP, HALF], F32, name=f"z{h}")
+            for r in range(TOP):
+                nc.vector.tensor_tensor(
+                    z[:, r, :],
+                    y[:].indirect(token_slots[r][:, h * HALF // 16 : (h + 1) * HALF // 16]),
+                    gates[:, r, cols],
+                    ALU.mult,
+                )
+            two = keep.tile([P, 2, HALF], F32, name=f"two{h}")
+            nc.vector.tensor_tensor(two[:], z[:, 0:2, :], z[:, 2:4, :], ALU.add)
+            nc.vector.tensor_tensor(ys[:, cols], ys[:, cols], two[:, 0, :], ALU.add)
+            nc.vector.tensor_tensor(ys[:, cols], ys[:, cols], two[:, 1, :], ALU.add)
+            nc.sync.dma_start(out[:, cols], ys[:, cols])

@@ -25,6 +25,10 @@ GROUP = 128
 SPARE = 1024
 WINDOW = T + SPARE
 HALF = T // 2
+AHEAD = 3
+LAG = 2
+SCALAR_SLOTS = 1792
+SHARED_AFTER = (0, 4, 5, 6)
 
 
 def tile_moe_shr_lin_relu_kernel(
@@ -34,14 +38,14 @@ def tile_moe_shr_lin_relu_kernel(
     with ExitStack() as ctx:
         keep = ctx.enter_context(tc.tile_pool(name="keep", bufs=1))
         ring = ctx.enter_context(tc.tile_pool(name="ring", bufs=3))
-        banks = ctx.enter_context(tc.psum_pool(name="banks", bufs=6))
+        banks = ctx.enter_context(tc.psum_pool(name="banks", bufs=7))
         shared_bank = ctx.enter_context(tc.psum_pool(name="shared_bank", bufs=1))
 
         x_rows = xT.rearrange("(a p u j) t -> a u p j t", a=PASSES, p=P, u=2, j=2)
         raw = []
         slot_tokens = keep.tile([P, SLOTS // 16], U16, name="slot_tokens")
         for i in range(PLANES):
-            tile = keep.tile([P, 2, T], F32, name=f"raw{i}")
+            tile = keep.tile([P, 2, T], F32, name=f"raw{i}", tag=f"stage{PLANES - 1 - i}", align_bytes=64)
             nc.sync.dma_start(tile[:], x_rows[i // 2, 1 - i % 2])
             raw.append(tile)
             if i == 0:
@@ -90,12 +94,15 @@ def tile_moe_shr_lin_relu_kernel(
         y = keep.tile([P, SLOTS], F32, name="y")
         ys = keep.tile([P, T], F32, name="ys")
 
-        chunks = []
-        for a in range(PASSES - 1):
-            chunks += [(a, 0, 1024), (a, 1024, 1024)]
-        chunks += [(3, 0, 512), (3, 512, 512), (3, 1024, 512), (3, 1536, 256), (3, 1792, 256)]
+        singles = keep.tile([P, 3 * T], BF16, name="singles", align_bytes=64)
+        nc.gpsimd.memset(singles[:, 2 * T :], 0.0)
+        nc.scalar.activation(singles[:, : 2 * T], raw[PLANES - 1][:].rearrange("p j t -> p (j t)"), ACT.Copy)
+
+        chunks = [((0,), 0, 1024), ((0,), 1024, 1024), ((1,), 0, 1024), ((1,), 1024, 1024)]
+        chunks += [((2, 3), 0, 512), ((2, 3), 512, 512), ((2, 3), 1024, 512), ((2, 3), 1536, 256), ((2, 3), 1792, 256)]
 
         made = {}
+        gathered = {}
 
         def multiply(acc, e, a, codes, scales):
             nc.tensor.matmul_mx(
@@ -108,34 +115,59 @@ def tile_moe_shr_lin_relu_kernel(
                 stop=(a == PASSES - 1),
             )
 
-        for number, (a, s0, n) in enumerate(chunks):
-            picked = ring.tile([P, 2, n], U32, name="picked", tag="picked", align_bytes=64)
-            for v in range(2):
-                i = 2 * a + v
-                window = pairs[:, plane_start(i) : plane_start(i) + WINDOW]
-                nc.vector.tensor_copy(picked[:, 1 - v, :], window.indirect(slot_tokens[:, s0 // 16 : (s0 + n) // 16]))
-            words = ring.tile([P, n, 2], U32, name="words", tag="words", align_bytes=64)
-            nc.scalar.copy(words[:], picked[:].rearrange("p u s -> p s u"))
-            codes = keep.tile([P, n], U32, name=f"codes{number}", align_bytes=64)
-            scales = keep.tile([P, n], U8, name=f"scales{number}", align_bytes=64)
-            nc.vector.quantize_mx(
-                out=codes[:].bitcast(FP8X4),
-                scales=scales[:],
-                in_=words[:].rearrange("p s u -> p (s u)").bitcast(BF16),
-            )
-            for slot in range(s0, s0 + n, GROUP):
-                cols = slice(slot - s0, slot - s0 + GROUP)
-                made[(a, slot)] = (codes[:, cols], scales[:, cols])
-            if s0 == 0:
-                tile, both = shared_words[a]
-                nc.scalar.copy(tile[:], both)
-            if a == PASSES - 1:
+        def gather(number):
+            passes, s0, n = chunks[number]
+            picked = ring.tile([P, 2 * n * len(passes)], U32, name="picked", tag="picked", align_bytes=64)
+            tokens = slot_tokens[:, s0 // 16 : (s0 + n) // 16]
+            for m, a in enumerate(passes):
+                for v in range(2):
+                    i = 2 * a + v
+                    dst = picked[:, (2 * m + 1 - v) * n : (2 * m + 2 - v) * n]
+                    if i == PLANES - 1 and s0 + n <= SCALAR_SLOTS:
+                        halves = dst.bitcast(BF16).rearrange("p (s j) -> p j s", j=2)
+                        for j in range(2):
+                            window = singles[:, j * T : (j + 2) * T]
+                            nc.scalar.activation(halves[:, j, :], window.indirect(tokens), ACT.Copy)
+                    else:
+                        window = pairs[:, plane_start(i) : plane_start(i) + WINDOW]
+                        nc.vector.tensor_copy(dst, window.indirect(tokens))
+            gathered[number] = picked
+
+        def finish(number):
+            passes, s0, n = chunks[number]
+            if PASSES - 1 in passes:
                 for slot in range(s0, s0 + n, GROUP):
                     e = slot // C
                     acc = banks.tile([P, GROUP], F32, name="acc")
                     for a2 in range(PASSES):
                         multiply(acc[:], e, a2, *made[(a2, slot)])
                     nc.scalar.activation(y[:, slot : slot + GROUP], acc[:], ACT.Relu, bias=bias[:, e : e + 1])
+
+        for number in range(AHEAD):
+            gather(number)
+        for number, (passes, s0, n) in enumerate(chunks):
+            width = n * len(passes)
+            words = keep.tile([P, 2 * width], U32, name="words", tag=f"stage{number % AHEAD}", align_bytes=64)
+            nc.scalar.copy(
+                words[:].rearrange("p (m s u) -> p m s u", m=len(passes), u=2),
+                gathered[number][:].rearrange("p (m u s) -> p m s u", m=len(passes), u=2),
+            )
+            codes = keep.tile([P, width], U32, name=f"codes{number}", align_bytes=64)
+            scales = keep.tile([P, width], U8, name=f"scales{number}", align_bytes=64)
+            nc.vector.quantize_mx(out=codes[:].bitcast(FP8X4), scales=scales[:], in_=words[:].bitcast(BF16))
+            for m, a in enumerate(passes):
+                for slot in range(s0, s0 + n, GROUP):
+                    cols = slice(m * n + slot - s0, m * n + slot - s0 + GROUP)
+                    made[(a, slot)] = (codes[:, cols], scales[:, cols])
+            if number + AHEAD < len(chunks):
+                gather(number + AHEAD)
+            if number in SHARED_AFTER:
+                tile, both = shared_words[SHARED_AFTER.index(number)]
+                nc.scalar.copy(tile[:], both)
+            if number >= LAG:
+                finish(number - LAG)
+        for number in range(len(chunks) - LAG, len(chunks)):
+            finish(number)
 
         acc = shared_bank.tile([P, T], F32, name="shared_acc")
         for a in range(PASSES):

@@ -1,6 +1,7 @@
 from contextlib import ExitStack
 
 import concourse.mybir as mybir
+from concourse.masks import make_identity
 
 K, T, E, C, N = 2048, 512, 8, 256, 128
 TOP = 4
@@ -25,10 +26,13 @@ GROUP = 128
 SPARE = 1024
 WINDOW = T + SPARE
 HALF = T // 2
-AHEAD = 3
+AHEAD = 4
 LAG = 2
-SCALAR_SLOTS = 1792
-SHARED_AFTER = (0, 4, 5, 6)
+STAGES = 3
+SCALAR_SLOTS = {5: 1024, 7: 2048}
+SCALAR_CASTS = 6
+BLOCKS = 3
+TURNED = BLOCKS * P
 
 
 def tile_moe_shr_lin_relu_kernel(
@@ -37,22 +41,30 @@ def tile_moe_shr_lin_relu_kernel(
     nc = tc.nc
     with ExitStack() as ctx:
         keep = ctx.enter_context(tc.tile_pool(name="keep", bufs=1))
-        ring = ctx.enter_context(tc.tile_pool(name="ring", bufs=3))
+        ring = ctx.enter_context(tc.tile_pool(name="ring", bufs=AHEAD))
         banks = ctx.enter_context(tc.psum_pool(name="banks", bufs=7))
         shared_bank = ctx.enter_context(tc.psum_pool(name="shared_bank", bufs=1))
 
         x_rows = xT.rearrange("(a p u j) t -> a u p j t", a=PASSES, p=P, u=2, j=2)
-        raw = []
         slot_tokens = keep.tile([P, SLOTS // 16], U16, name="slot_tokens")
-        for i in range(PLANES):
-            tile = keep.tile([P, 2, T], F32, name=f"raw{i}", tag=f"stage{PLANES - 1 - i}", align_bytes=64)
-            nc.sync.dma_start(tile[:], x_rows[i // 2, 1 - i % 2])
-            raw.append(tile)
-            if i == 0:
-                nc.sync.dma_start(slot_tokens[:], offs)
+        raw = []
+        for a in range(PASSES):
+            raw.append(keep.tile([P, 4 * T], F32, name=f"raw{a}"))
 
-        pairs = keep.tile([P, PLANES * T + SPARE], U32, name="pairs", align_bytes=64)
-        nc.vector.memset(pairs[:, PLANES * T :], 0)
+        def raw_plane(i):
+            u = 1 - i % 2
+            return raw[i // 2][:, 2 * u * T : 2 * (u + 1) * T].rearrange("p (j t) -> p j t", j=2)
+
+        for h in range(2):
+            cols = slice(h * HALF, (h + 1) * HALF)
+            nc.sync.dma_start(raw_plane(0)[:, :, cols], x_rows[0, 1][:, :, cols])
+        nc.sync.dma_start(slot_tokens[:], offs)
+        for i in range(1, PLANES):
+            nc.sync.dma_start(raw_plane(i), x_rows[i // 2, 1 - i % 2])
+
+        paired = [i for i in range(PLANES) if SCALAR_SLOTS.get(i, 0) < SLOTS]
+        pairs = keep.tile([P, len(paired) * T + SPARE], U32, name="pairs", align_bytes=64)
+        nc.vector.memset(pairs[:, len(paired) * T :], 0)
         w_scale = keep.tile([P, (E + 1) * PASSES, N], U8, name="w_scale", align_bytes=64)
         nc.gpsimd.memset(w_scale[:].bitcast(I32), 0)
         w_code = keep.tile([P, (E + 1) * PASSES, 2 * N], U8, name="w_code", align_bytes=64)
@@ -62,8 +74,16 @@ def tile_moe_shr_lin_relu_kernel(
             nc.sync.dma_start(w_scale[r:P:32, :, :].bitcast(I32), scale_rows[r].bitcast(I32))
         bias = keep.tile([P, E + 1], F32, name="bias")
         nc.sync.dma_start(bias[:], b)
-        gates = keep.tile([P, TOP, T], F32, name="gates")
-        nc.sync.dma_start(gates[:], gate.rearrange("r p t -> p r t"))
+        gates = keep.tile([P, TOP, T - TURNED], F32, name="gates")
+        nc.sync.dma_start(gates[:], gate.rearrange("r p t -> p r t")[:, :, TURNED:])
+        token_gates = []
+        for r in range(TOP):
+            tile = keep.tile([P, BLOCKS], F32, name=f"token_gates{r}")
+            with nc.allow_non_contiguous_dma(reason="one gate value a partition"):
+                nc.sync.dma_start(tile[:], gate[r, 0, :TURNED].rearrange("(k p) -> p k", p=P))
+            token_gates.append(tile)
+        identity = keep.tile([P, P], F32, name="identity")
+        make_identity(nc, identity[:])
         token_slots = []
         for r, pos in enumerate((pos1, pos2, pos3, pos4)):
             tile = keep.tile([P, T // 16], U16, name=f"token_slots{r}")
@@ -71,32 +91,41 @@ def tile_moe_shr_lin_relu_kernel(
             token_slots.append(tile)
 
         def plane_start(i):
-            return (PLANES - 1 - i) * T
+            return (len(paired) - 1 - paired.index(i)) * T
 
-        def cast_plane(i):
-            dst = pairs[:, plane_start(i) : plane_start(i) + T].bitcast(BF16).rearrange("p (t j) -> p t j", j=2)
-            src = raw[i][:].rearrange("p j t -> p t j")
-            if i == 0:
-                nc.vector.tensor_copy(dst, src)
-            else:
-                nc.scalar.activation(dst, src, ACT.Copy)
+        def pair_view(i):
+            return pairs[:, plane_start(i) : plane_start(i) + T].bitcast(BF16).rearrange("p (t j) -> p t j", j=2)
 
-        for i in range(PLANES):
-            cast_plane(i)
+        def gpsimd_cast(dst, src):
+            nc.gpsimd.tensor_scalar(dst, src, 1.0, 0.0, ALU.mult, ALU.add)
 
+        for h in range(2):
+            cols = slice(h * HALF, (h + 1) * HALF)
+            nc.vector.tensor_copy(pair_view(0)[:, cols, :], raw_plane(0).rearrange("p j t -> p t j")[:, cols, :])
+        for i in range(1, SCALAR_CASTS):
+            nc.scalar.activation(pair_view(i), raw_plane(i).rearrange("p j t -> p t j"), ACT.Copy)
+
+        singles = keep.tile([P, (2 * len(SCALAR_SLOTS) + 1) * T], BF16, name="singles", align_bytes=64)
+        nc.gpsimd.memset(singles[:, 2 * len(SCALAR_SLOTS) * T :], 0.0)
+        single_start = {i: 2 * T * (len(SCALAR_SLOTS) - 1 - m) for m, i in enumerate(sorted(SCALAR_SLOTS))}
         shared_words = []
         for a in range(PASSES):
-            tile = keep.tile([P, T, 2], U32, name=f"shared_words{a}", align_bytes=64)
-            lo = plane_start(2 * a + 1)
-            both = pairs[:, lo : lo + 2 * T].rearrange("p (u t) -> p t u", u=2)
-            shared_words.append((tile, both))
+            shared_words.append(keep.tile([P, T, 4], BF16, name=f"shared_words{a}", align_bytes=64))
+
+        def cast_shared(a):
+            gpsimd_cast(shared_words[a][:], raw[a][:].rearrange("p (j t) -> p t j", j=4))
+
+        cast_shared(0)
+        cast_shared(1)
+        for i in sorted(SCALAR_SLOTS):
+            gpsimd_cast(singles[:, single_start[i] : single_start[i] + 2 * T], raw_plane(i).rearrange("p j t -> p (j t)"))
+        for i in paired[SCALAR_CASTS:]:
+            gpsimd_cast(pair_view(i), raw_plane(i).rearrange("p j t -> p t j"))
+        cast_shared(2)
+        cast_shared(3)
 
         y = keep.tile([P, SLOTS], F32, name="y")
         ys = keep.tile([P, T], F32, name="ys")
-
-        singles = keep.tile([P, 3 * T], BF16, name="singles", align_bytes=64)
-        nc.gpsimd.memset(singles[:, 2 * T :], 0.0)
-        nc.scalar.activation(singles[:, : 2 * T], raw[PLANES - 1][:].rearrange("p j t -> p (j t)"), ACT.Copy)
 
         chunks = [((0,), 0, 1024), ((0,), 1024, 1024), ((1,), 0, 1024), ((1,), 1024, 1024)]
         chunks += [((2, 3), 0, 512), ((2, 3), 512, 512), ((2, 3), 1024, 512), ((2, 3), 1536, 256), ((2, 3), 1792, 256)]
@@ -123,10 +152,10 @@ def tile_moe_shr_lin_relu_kernel(
                 for v in range(2):
                     i = 2 * a + v
                     dst = picked[:, (2 * m + 1 - v) * n : (2 * m + 2 - v) * n]
-                    if i == PLANES - 1 and s0 + n <= SCALAR_SLOTS:
+                    if s0 + n <= SCALAR_SLOTS.get(i, 0):
                         halves = dst.bitcast(BF16).rearrange("p (s j) -> p j s", j=2)
                         for j in range(2):
-                            window = singles[:, j * T : (j + 2) * T]
+                            window = singles[:, single_start[i] + j * T : single_start[i] + (j + 2) * T]
                             nc.scalar.activation(halves[:, j, :], window.indirect(tokens), ACT.Copy)
                     else:
                         window = pairs[:, plane_start(i) : plane_start(i) + WINDOW]
@@ -147,7 +176,7 @@ def tile_moe_shr_lin_relu_kernel(
             gather(number)
         for number, (passes, s0, n) in enumerate(chunks):
             width = n * len(passes)
-            words = keep.tile([P, 2 * width], U32, name="words", tag=f"stage{number % AHEAD}", align_bytes=64)
+            words = keep.tile([P, 2 * width], U32, name="words", tag=f"stage{number % STAGES}", align_bytes=64)
             nc.scalar.copy(
                 words[:].rearrange("p (m s u) -> p m s u", m=len(passes), u=2),
                 gathered[number][:].rearrange("p (m u s) -> p m s u", m=len(passes), u=2),
@@ -161,9 +190,6 @@ def tile_moe_shr_lin_relu_kernel(
                     made[(a, slot)] = (codes[:, cols], scales[:, cols])
             if number + AHEAD < len(chunks):
                 gather(number + AHEAD)
-            if number in SHARED_AFTER:
-                tile, both = shared_words[SHARED_AFTER.index(number)]
-                nc.scalar.copy(tile[:], both)
             if number >= LAG:
                 finish(number - LAG)
         for number in range(len(chunks) - LAG, len(chunks)):
@@ -176,23 +202,46 @@ def tile_moe_shr_lin_relu_kernel(
             nc.vector.quantize_mx(
                 out=codes[:].bitcast(FP8X4),
                 scales=scales[:],
-                in_=shared_words[a][0][:].rearrange("p s u -> p (s u)").bitcast(BF16),
+                in_=shared_words[a][:].rearrange("p t j -> p (t j)"),
             )
             multiply(acc[:], E, a, codes[:], scales[:])
         nc.scalar.activation(ys[:], acc[:], ACT.Relu, bias=bias[:, E : E + 1])
 
-        for h in range(2):
-            cols = slice(h * HALF, (h + 1) * HALF)
-            z = keep.tile([P, TOP, HALF], F32, name=f"z{h}")
-            for r in range(TOP):
-                nc.vector.tensor_tensor(
-                    z[:, r, :],
-                    y[:].indirect(token_slots[r][:, h * HALF // 16 : (h + 1) * HALF // 16]),
-                    gates[:, r, cols],
-                    ALU.mult,
-                )
-            two = keep.tile([P, 2, HALF], F32, name=f"two{h}")
-            nc.vector.tensor_tensor(two[:], z[:, 0:2, :], z[:, 2:4, :], ALU.add)
-            nc.vector.tensor_tensor(ys[:, cols], ys[:, cols], two[:, 0, :], ALU.add)
-            nc.vector.tensor_tensor(ys[:, cols], ys[:, cols], two[:, 1, :], ALU.add)
-            nc.sync.dma_start(out[:, cols], ys[:, cols])
+        def add_turned(acc, src, first, last):
+            nc.tensor.matmul(acc, lhsT=src, rhs=identity[:], start=first, stop=last, is_transpose=True)
+
+        def turn(src):
+            bank = banks.tile([P, BLOCKS, P], F32, name="bank", tag="acc")
+            for k in range(BLOCKS):
+                nc.tensor.transpose(bank[:, k, :], src[:, k * P : (k + 1) * P], identity[:])
+            return bank
+
+        picked_y = keep.tile([P, TOP, TURNED], F32, name="picked_y")
+        for r in range(TOP):
+            nc.vector.tensor_copy(picked_y[:, r, :], y[:].indirect(token_slots[r][:, : TURNED // 16]))
+        terms = keep.tile([P, TOP + 1, BLOCKS, P], F32, name="terms")
+        nc.scalar.copy(terms[:, TOP, :, :], turn(ys[:])[:])
+        sums = []
+        for k in range(BLOCKS):
+            total = banks.tile([P, P], F32, name="total", tag="acc")
+            add_turned(total[:], terms[:, TOP, k, :], True, False)
+            sums.append(total)
+        for r in range(TOP):
+            bank = turn(picked_y[:, r, :])
+            for k in range(BLOCKS):
+                nc.scalar.activation(terms[:, r, k, :], bank[:, k, :], ACT.Copy, scale=token_gates[r][:, k : k + 1])
+                add_turned(sums[k][:], terms[:, r, k, :], False, r == TOP - 1)
+        result = keep.tile([P, TURNED], F32, name="result")
+        for k in range(BLOCKS):
+            nc.scalar.copy(result[:, k * P : (k + 1) * P], sums[k][:])
+        nc.sync.dma_start(out[:, :TURNED], result[:])
+
+        z = keep.tile([P, TOP, T - TURNED], F32, name="z")
+        for r in range(TOP):
+            nc.vector.tensor_tensor(z[:, r, :], y[:].indirect(token_slots[r][:, TURNED // 16 :]), gates[:, r, :], ALU.mult)
+        two = keep.tile([P, 2, T - TURNED], F32, name="two")
+        nc.vector.tensor_tensor(two[:], z[:, 0:2, :], z[:, 2:4, :], ALU.add)
+        rest = keep.tile([P, T - TURNED], F32, name="rest")
+        nc.vector.tensor_tensor(rest[:], ys[:, TURNED:], two[:, 0, :], ALU.add)
+        nc.vector.tensor_tensor(rest[:], rest[:], two[:, 1, :], ALU.add)
+        nc.sync.dma_start(out[:, TURNED:], rest[:])

@@ -23,14 +23,16 @@ P = 128
 PASSES = K // (4 * P)
 PLANES = 2 * PASSES
 GROUP = 128
-SPARE = 1024
+SPARE = T
 WINDOW = T + SPARE
 HALF = T // 2
 AHEAD = 4
 LAG = 2
 STAGES = 3
-SCALAR_SLOTS = {5: 1024, 7: 2048}
-SCALAR_CASTS = 6
+SCALAR_PLANES = (1, 7)
+CHUNK = 512
+GPSIMD_WEAVES = 6
+VECTOR_WEAVES = 4
 BLOCKS = 3
 TURNED = BLOCKS * P
 
@@ -41,7 +43,6 @@ def tile_moe_shr_lin_relu_kernel(
     nc = tc.nc
     with ExitStack() as ctx:
         keep = ctx.enter_context(tc.tile_pool(name="keep", bufs=1))
-        ring = ctx.enter_context(tc.tile_pool(name="ring", bufs=AHEAD))
         banks = ctx.enter_context(tc.psum_pool(name="banks", bufs=7))
         shared_bank = ctx.enter_context(tc.psum_pool(name="shared_bank", bufs=1))
 
@@ -59,10 +60,12 @@ def tile_moe_shr_lin_relu_kernel(
             cols = slice(h * HALF, (h + 1) * HALF)
             nc.sync.dma_start(raw_plane(0)[:, :, cols], x_rows[0, 1][:, :, cols])
         nc.sync.dma_start(slot_tokens[:], offs)
-        for i in range(1, PLANES):
+        for j in (1, 0):
+            nc.sync.dma_start(raw_plane(1)[:, j, :], x_rows[0, 0][:, j, :])
+        for i in range(2, PLANES):
             nc.sync.dma_start(raw_plane(i), x_rows[i // 2, 1 - i % 2])
 
-        paired = [i for i in range(PLANES) if SCALAR_SLOTS.get(i, 0) < SLOTS]
+        paired = [i for i in range(PLANES) if i not in SCALAR_PLANES]
         pairs = keep.tile([P, len(paired) * T + SPARE], U32, name="pairs", align_bytes=64)
         nc.vector.memset(pairs[:, len(paired) * T :], 0)
         w_scale = keep.tile([P, (E + 1) * PASSES, N], U8, name="w_scale", align_bytes=64)
@@ -102,36 +105,38 @@ def tile_moe_shr_lin_relu_kernel(
         for h in range(2):
             cols = slice(h * HALF, (h + 1) * HALF)
             nc.vector.tensor_copy(pair_view(0)[:, cols, :], raw_plane(0).rearrange("p j t -> p t j")[:, cols, :])
-        for i in range(1, SCALAR_CASTS):
-            nc.scalar.activation(pair_view(i), raw_plane(i).rearrange("p j t -> p t j"), ACT.Copy)
 
-        singles = keep.tile([P, (2 * len(SCALAR_SLOTS) + 1) * T], BF16, name="singles", align_bytes=64)
-        nc.gpsimd.memset(singles[:, 2 * len(SCALAR_SLOTS) * T :], 0.0)
-        single_start = {i: 2 * T * (len(SCALAR_SLOTS) - 1 - m) for m, i in enumerate(sorted(SCALAR_SLOTS))}
-        shared_words = []
-        for a in range(PASSES):
-            shared_words.append(keep.tile([P, T, 4], BF16, name=f"shared_words{a}", align_bytes=64))
+        singles = keep.tile([P, (2 * len(SCALAR_PLANES) + 1) * T], BF16, name="singles", align_bytes=64)
+        nc.gpsimd.memset(singles[:, 2 * len(SCALAR_PLANES) * T :], 0.0)
+        single_start = {i: 2 * T * (len(SCALAR_PLANES) - 1 - m) for m, i in enumerate(SCALAR_PLANES)}
 
-        def cast_shared(a):
-            gpsimd_cast(shared_words[a][:], raw[a][:].rearrange("p (j t) -> p t j", j=4))
+        def single_rows(i):
+            return singles[:, single_start[i] : single_start[i] + 2 * T], raw_plane(i).rearrange("p j t -> p (j t)")
 
-        cast_shared(0)
-        cast_shared(1)
-        for i in sorted(SCALAR_SLOTS):
-            gpsimd_cast(singles[:, single_start[i] : single_start[i] + 2 * T], raw_plane(i).rearrange("p j t -> p (j t)"))
-        for i in paired[SCALAR_CASTS:]:
+        dst, src = single_rows(SCALAR_PLANES[0])
+        nc.scalar.activation(dst[:, T:], src[:, T:], ACT.Copy)
+        gpsimd_cast(dst[:, :T], src[:, :T])
+        for i in paired[1:]:
             gpsimd_cast(pair_view(i), raw_plane(i).rearrange("p j t -> p t j"))
-        cast_shared(2)
-        cast_shared(3)
+        gpsimd_cast(*single_rows(SCALAR_PLANES[1]))
+
+        shared_words = {}
+
+        def cast_shared(a, tag):
+            tile = keep.tile([P, T, 4], BF16, name=f"shared_words{a}", tag=tag, align_bytes=64)
+            gpsimd_cast(tile[:], raw[a][:].rearrange("p (j t) -> p t j", j=4))
+            shared_words[a] = tile
+
+        cast_shared(PASSES - 1, "shared_words")
 
         y = keep.tile([P, SLOTS], F32, name="y")
         ys = keep.tile([P, T], F32, name="ys")
 
-        chunks = [((0,), 0, 1024), ((0,), 1024, 1024), ((1,), 0, 1024), ((1,), 1024, 1024)]
-        chunks += [((2, 3), 0, 512), ((2, 3), 512, 512), ((2, 3), 1024, 512), ((2, 3), 1536, 256), ((2, 3), 1792, 256)]
+        chunks = [(passes, s0, CHUNK) for passes in ((0, 1), (2, 3)) for s0 in range(0, SLOTS, CHUNK)]
 
         made = {}
         gathered = {}
+        places = {}
 
         def multiply(acc, e, a, codes, scales):
             nc.tensor.matmul_mx(
@@ -144,43 +149,69 @@ def tile_moe_shr_lin_relu_kernel(
                 stop=(a == PASSES - 1),
             )
 
-        def gather(number):
+        def gather(number, place):
             passes, s0, n = chunks[number]
-            picked = ring.tile([P, 2 * n * len(passes)], U32, name="picked", tag="picked", align_bytes=64)
+            picked = keep.tile([P, 2 * n * len(passes)], U32, name="picked", tag=f"picked{place}", align_bytes=64)
             tokens = slot_tokens[:, s0 // 16 : (s0 + n) // 16]
             for m, a in enumerate(passes):
                 for v in range(2):
                     i = 2 * a + v
                     dst = picked[:, (2 * m + 1 - v) * n : (2 * m + 2 - v) * n]
-                    if s0 + n <= SCALAR_SLOTS.get(i, 0):
+                    if i in SCALAR_PLANES:
                         halves = dst.bitcast(BF16).rearrange("p (s j) -> p j s", j=2)
-                        for j in range(2):
+                        for j in (1, 0):
                             window = singles[:, single_start[i] + j * T : single_start[i] + (j + 2) * T]
                             nc.scalar.activation(halves[:, j, :], window.indirect(tokens), ACT.Copy)
                     else:
                         window = pairs[:, plane_start(i) : plane_start(i) + WINDOW]
                         nc.vector.tensor_copy(dst, window.indirect(tokens))
             gathered[number] = picked
+            places[number] = place
 
         def finish(number):
             passes, s0, n = chunks[number]
             if PASSES - 1 in passes:
-                for slot in range(s0, s0 + n, GROUP):
-                    e = slot // C
-                    acc = banks.tile([P, GROUP], F32, name="acc")
-                    for a2 in range(PASSES):
-                        multiply(acc[:], e, a2, *made[(a2, slot)])
-                    nc.scalar.activation(y[:, slot : slot + GROUP], acc[:], ACT.Relu, bias=bias[:, e : e + 1])
+                width = GROUP if number >= len(chunks) - 2 else C
+                for first in range(s0, s0 + n, width):
+                    e = first // C
+                    acc = banks.tile([P, width], F32, name="acc")
+                    for slot in range(first, first + width, GROUP):
+                        for a2 in range(PASSES):
+                            multiply(acc[:, slot - first : slot - first + GROUP], e, a2, *made[(a2, slot)])
+                    nc.scalar.activation(y[:, first : first + width], acc[:], ACT.Relu, bias=bias[:, e : e + 1])
 
         for number in range(AHEAD):
-            gather(number)
-        for number, (passes, s0, n) in enumerate(chunks):
+            gather(number, number)
+        half = len(chunks) // 2
+        order = [0]
+        for j in range(half - 1):
+            order.extend([j + 1, half + j])
+        order.append(len(chunks) - 1)
+        for step, number in enumerate(order):
+            passes, s0, n = chunks[number]
             width = n * len(passes)
-            words = keep.tile([P, 2 * width], U32, name="words", tag=f"stage{number % STAGES}", align_bytes=64)
-            nc.scalar.copy(
-                words[:].rearrange("p (m s u) -> p m s u", m=len(passes), u=2),
-                gathered[number][:].rearrange("p (m u s) -> p m s u", m=len(passes), u=2),
-            )
+            tag = f"early{step}" if step < PASSES - 1 else f"stage{step % STAGES}"
+            words = keep.tile([P, 2 * width], U32, name="words", tag=tag, align_bytes=64)
+            if number in (GPSIMD_WEAVES, VECTOR_WEAVES):
+                if number == GPSIMD_WEAVES:
+                    gpsimd_cast(
+                        words[:, :width].bitcast(BF16).rearrange("p (s u j) -> p s u j", u=2, j=2),
+                        gathered[number][:, :width].bitcast(BF16).rearrange("p (u s j) -> p s u j", u=2, j=2),
+                    )
+                else:
+                    nc.vector.tensor_copy(
+                        words[:, :width].bitcast(I32).rearrange("p (s u) -> p s u", u=2),
+                        gathered[number][:, :width].bitcast(I32).rearrange("p (u s) -> p s u", u=2),
+                    )
+                nc.scalar.copy(
+                    words[:, width:].rearrange("p (s u) -> p s u", u=2),
+                    gathered[number][:, width:].rearrange("p (u s) -> p s u", u=2),
+                )
+            else:
+                nc.scalar.copy(
+                    words[:].rearrange("p (m s u) -> p m s u", m=len(passes), u=2),
+                    gathered[number][:].rearrange("p (m u s) -> p m s u", m=len(passes), u=2),
+                )
             codes = keep.tile([P, width], U32, name=f"codes{number}", align_bytes=64)
             scales = keep.tile([P, width], U8, name=f"scales{number}", align_bytes=64)
             nc.vector.quantize_mx(out=codes[:].bitcast(FP8X4), scales=scales[:], in_=words[:].bitcast(BF16))
@@ -188,23 +219,28 @@ def tile_moe_shr_lin_relu_kernel(
                 for slot in range(s0, s0 + n, GROUP):
                     cols = slice(m * n + slot - s0, m * n + slot - s0 + GROUP)
                     made[(a, slot)] = (codes[:, cols], scales[:, cols])
-            if number + AHEAD < len(chunks):
-                gather(number + AHEAD)
-            if number >= LAG:
-                finish(number - LAG)
-        for number in range(len(chunks) - LAG, len(chunks)):
+            if step < PASSES - 1:
+                cast_shared(step, tag)
+            if step + AHEAD < len(chunks):
+                gather(step + AHEAD, places[number])
+            if step >= LAG:
+                finish(order[step - LAG])
+        for number in order[-LAG:]:
             finish(number)
 
         acc = shared_bank.tile([P, T], F32, name="shared_acc")
+        last = len(chunks) - 1
+        codes_first = keep.tile([P, T], U32, name="codes_first", tag=f"picked{places[last - 1]}", align_bytes=64)
+        codes_rest = keep.tile([P, (PASSES - 1) * T], U32, name="codes_rest", tag=f"picked{places[last]}", align_bytes=64)
         for a in range(PASSES):
-            codes = ring.tile([P, T], U32, name="shared_codes", tag="picked", align_bytes=64)
+            codes = codes_first[:] if a == 0 else codes_rest[:, (a - 1) * T : a * T]
             scales = keep.tile([P, T], U8, name=f"shared_scales{a}", align_bytes=64)
             nc.vector.quantize_mx(
-                out=codes[:].bitcast(FP8X4),
+                out=codes.bitcast(FP8X4),
                 scales=scales[:],
                 in_=shared_words[a][:].rearrange("p t j -> p (t j)"),
             )
-            multiply(acc[:], E, a, codes[:], scales[:])
+            multiply(acc[:], E, a, codes, scales[:])
         nc.scalar.activation(ys[:], acc[:], ACT.Relu, bias=bias[:, E : E + 1])
 
         def add_turned(acc, src, first, last):
@@ -220,28 +256,30 @@ def tile_moe_shr_lin_relu_kernel(
         for r in range(TOP):
             nc.vector.tensor_copy(picked_y[:, r, :], y[:].indirect(token_slots[r][:, : TURNED // 16]))
         terms = keep.tile([P, TOP + 1, BLOCKS, P], F32, name="terms")
-        nc.scalar.copy(terms[:, TOP, :, :], turn(ys[:])[:])
         sums = []
         for k in range(BLOCKS):
-            total = banks.tile([P, P], F32, name="total", tag="acc")
-            add_turned(total[:], terms[:, TOP, k, :], True, False)
-            sums.append(total)
+            sums.append(banks.tile([P, P], F32, name="total", tag="acc"))
         for r in range(TOP):
             bank = turn(picked_y[:, r, :])
             for k in range(BLOCKS):
                 nc.scalar.activation(terms[:, r, k, :], bank[:, k, :], ACT.Copy, scale=token_gates[r][:, k : k + 1])
-                add_turned(sums[k][:], terms[:, r, k, :], False, r == TOP - 1)
+                add_turned(sums[k][:], terms[:, r, k, :], r == 0, r == TOP - 1)
+            if r == 0:
+                nc.scalar.copy(terms[:, TOP, :, :], turn(ys[:])[:])
+                for k in range(BLOCKS):
+                    add_turned(sums[k][:], terms[:, TOP, k, :], False, False)
         result = keep.tile([P, TURNED], F32, name="result")
         for k in range(BLOCKS):
             nc.scalar.copy(result[:, k * P : (k + 1) * P], sums[k][:])
         nc.sync.dma_start(out[:, :TURNED], result[:])
 
         z = keep.tile([P, TOP, T - TURNED], F32, name="z")
-        for r in range(TOP):
-            nc.vector.tensor_tensor(z[:, r, :], y[:].indirect(token_slots[r][:, TURNED // 16 :]), gates[:, r, :], ALU.mult)
-        two = keep.tile([P, 2, T - TURNED], F32, name="two")
-        nc.vector.tensor_tensor(two[:], z[:, 0:2, :], z[:, 2:4, :], ALU.add)
         rest = keep.tile([P, T - TURNED], F32, name="rest")
-        nc.vector.tensor_tensor(rest[:], ys[:, TURNED:], two[:, 0, :], ALU.add)
-        nc.vector.tensor_tensor(rest[:], rest[:], two[:, 1, :], ALU.add)
+        for r in range(TOP + 1):
+            if r < TOP:
+                nc.vector.tensor_tensor(z[:, r, :], y[:].indirect(token_slots[r][:, TURNED // 16 :]), gates[:, r, :], ALU.mult)
+            if r == 1:
+                nc.vector.tensor_tensor(rest[:], ys[:, TURNED:], z[:, 0, :], ALU.add)
+            elif r > 1:
+                nc.vector.tensor_tensor(rest[:], rest[:], z[:, r - 1, :], ALU.add)
         nc.sync.dma_start(out[:, TURNED:], rest[:])

@@ -22,17 +22,23 @@ ALU = mybir.AluOpType
 P = 128
 PASSES = K // (4 * P)
 PLANES = 2 * PASSES
+PER_COLUMN = 16
 GROUP = 128
-SPARE = T
-WINDOW = T + SPARE
 HALF = T // 2
-AHEAD = 4
-LAG = 2
-STAGES = 3
-SCALAR_PLANES = (1, 7)
+
+SPARE = 2 * T
+WINDOW = T + SPARE
+
 CHUNK = 512
+AHEAD = 4
+STAGES = 3
+LAG = 2
+BANKS = 7
+
+SCALAR_PLANES = (1, PLANES - 1)
 GPSIMD_WEAVES = 6
 VECTOR_WEAVES = 4
+
 BLOCKS = 3
 TURNED = BLOCKS * P
 
@@ -43,11 +49,11 @@ def tile_moe_shr_lin_relu_kernel(
     nc = tc.nc
     with ExitStack() as ctx:
         keep = ctx.enter_context(tc.tile_pool(name="keep", bufs=1))
-        banks = ctx.enter_context(tc.psum_pool(name="banks", bufs=7))
+        banks = ctx.enter_context(tc.psum_pool(name="banks", bufs=BANKS))
         shared_bank = ctx.enter_context(tc.psum_pool(name="shared_bank", bufs=1))
 
         x_rows = xT.rearrange("(a p u j) t -> a u p j t", a=PASSES, p=P, u=2, j=2)
-        slot_tokens = keep.tile([P, SLOTS // 16], U16, name="slot_tokens")
+        slot_tokens = keep.tile([P, SLOTS // PER_COLUMN], U16, name="slot_tokens")
         raw = []
         for a in range(PASSES):
             raw.append(keep.tile([P, 4 * T], F32, name=f"raw{a}"))
@@ -68,6 +74,9 @@ def tile_moe_shr_lin_relu_kernel(
         paired = [i for i in range(PLANES) if i not in SCALAR_PLANES]
         pairs = keep.tile([P, len(paired) * T + SPARE], U32, name="pairs", align_bytes=64)
         nc.vector.memset(pairs[:, len(paired) * T :], 0)
+        singles = keep.tile([P, 2 * len(SCALAR_PLANES) * T + SPARE], BF16, name="singles", align_bytes=64)
+        nc.vector.memset(singles[:, 2 * len(SCALAR_PLANES) * T :], 0.0)
+
         w_scale = keep.tile([P, (E + 1) * PASSES, N], U8, name="w_scale", align_bytes=64)
         nc.gpsimd.memset(w_scale[:].bitcast(I32), 0)
         w_code = keep.tile([P, (E + 1) * PASSES, 2 * N], U8, name="w_code", align_bytes=64)
@@ -75,23 +84,24 @@ def tile_moe_shr_lin_relu_kernel(
         scale_rows = w_scales.rearrange("e a (q r) n -> r q (e a) n", r=4)
         for r in range(4):
             nc.sync.dma_start(w_scale[r:P:32, :, :].bitcast(I32), scale_rows[r].bitcast(I32))
+
         bias = keep.tile([P, E + 1], F32, name="bias")
         nc.sync.dma_start(bias[:], b)
         gates = keep.tile([P, TOP, T - TURNED], F32, name="gates")
         nc.sync.dma_start(gates[:], gate.rearrange("r p t -> p r t")[:, :, TURNED:])
         token_gates = []
         for r in range(TOP):
-            tile = keep.tile([P, BLOCKS], F32, name=f"token_gates{r}")
+            column = keep.tile([P, BLOCKS], F32, name=f"token_gates{r}")
             with nc.allow_non_contiguous_dma(reason="one gate value a partition"):
-                nc.sync.dma_start(tile[:], gate[r, 0, :TURNED].rearrange("(k p) -> p k", p=P))
-            token_gates.append(tile)
+                nc.sync.dma_start(column[:], gate[r, 0, :TURNED].rearrange("(k p) -> p k", p=P))
+            token_gates.append(column)
         identity = keep.tile([P, P], F32, name="identity")
         make_identity(nc, identity[:])
         token_slots = []
         for r, pos in enumerate((pos1, pos2, pos3, pos4)):
-            tile = keep.tile([P, T // 16], U16, name=f"token_slots{r}")
-            nc.sync.dma_start(tile[:], pos)
-            token_slots.append(tile)
+            inverse = keep.tile([P, T // PER_COLUMN], U16, name=f"token_slots{r}")
+            nc.sync.dma_start(inverse[:], pos)
+            token_slots.append(inverse)
 
         def plane_start(i):
             return (len(paired) - 1 - paired.index(i)) * T
@@ -99,40 +109,39 @@ def tile_moe_shr_lin_relu_kernel(
         def pair_view(i):
             return pairs[:, plane_start(i) : plane_start(i) + T].bitcast(BF16).rearrange("p (t j) -> p t j", j=2)
 
-        def gpsimd_cast(dst, src):
+        def gpsimd_copy(dst, src):
             nc.gpsimd.tensor_scalar(dst, src, 1.0, 0.0, ALU.mult, ALU.add)
 
         for h in range(2):
             cols = slice(h * HALF, (h + 1) * HALF)
             nc.vector.tensor_copy(pair_view(0)[:, cols, :], raw_plane(0).rearrange("p j t -> p t j")[:, cols, :])
 
-        singles = keep.tile([P, (2 * len(SCALAR_PLANES) + 1) * T], BF16, name="singles", align_bytes=64)
-        nc.gpsimd.memset(singles[:, 2 * len(SCALAR_PLANES) * T :], 0.0)
         single_start = {i: 2 * T * (len(SCALAR_PLANES) - 1 - m) for m, i in enumerate(SCALAR_PLANES)}
 
         def single_rows(i):
             return singles[:, single_start[i] : single_start[i] + 2 * T], raw_plane(i).rearrange("p j t -> p (j t)")
 
-        dst, src = single_rows(SCALAR_PLANES[0])
-        nc.scalar.activation(dst[:, T:], src[:, T:], ACT.Copy)
-        gpsimd_cast(dst[:, :T], src[:, :T])
+        rounded_rows, raw_rows = single_rows(SCALAR_PLANES[0])
+        nc.scalar.activation(rounded_rows[:, T:], raw_rows[:, T:], ACT.Copy)
+        gpsimd_copy(rounded_rows[:, :T], raw_rows[:, :T])
         for i in paired[1:]:
-            gpsimd_cast(pair_view(i), raw_plane(i).rearrange("p j t -> p t j"))
-        gpsimd_cast(*single_rows(SCALAR_PLANES[1]))
+            gpsimd_copy(pair_view(i), raw_plane(i).rearrange("p j t -> p t j"))
+        gpsimd_copy(*single_rows(SCALAR_PLANES[1]))
 
         shared_words = {}
 
-        def cast_shared(a, tag):
-            tile = keep.tile([P, T, 4], BF16, name=f"shared_words{a}", tag=tag, align_bytes=64)
-            gpsimd_cast(tile[:], raw[a][:].rearrange("p (j t) -> p t j", j=4))
-            shared_words[a] = tile
+        def round_shared(a, tag):
+            tokens_of_pass = keep.tile([P, T, 4], BF16, name=f"shared_words{a}", tag=tag, align_bytes=64)
+            gpsimd_copy(tokens_of_pass[:], raw[a][:].rearrange("p (d t) -> p t d", d=4))
+            shared_words[a] = tokens_of_pass
 
-        cast_shared(PASSES - 1, "shared_words")
+        round_shared(PASSES - 1, "shared_words")
 
         y = keep.tile([P, SLOTS], F32, name="y")
         ys = keep.tile([P, T], F32, name="ys")
 
-        chunks = [(passes, s0, CHUNK) for passes in ((0, 1), (2, 3)) for s0 in range(0, SLOTS, CHUNK)]
+        chunks = [((a,), s0, 2 * CHUNK) for s0 in range(0, SLOTS, 2 * CHUNK) for a in (0, 1)]
+        chunks.extend([((2, 3), s0, CHUNK) for s0 in range(0, SLOTS, CHUNK)])
 
         made = {}
         gathered = {}
@@ -152,7 +161,7 @@ def tile_moe_shr_lin_relu_kernel(
         def gather(number, place):
             passes, s0, n = chunks[number]
             picked = keep.tile([P, 2 * n * len(passes)], U32, name="picked", tag=f"picked{place}", align_bytes=64)
-            tokens = slot_tokens[:, s0 // 16 : (s0 + n) // 16]
+            tokens = slot_tokens[:, s0 // PER_COLUMN : (s0 + n) // PER_COLUMN]
             for m, a in enumerate(passes):
                 for v in range(2):
                     i = 2 * a + v
@@ -160,13 +169,38 @@ def tile_moe_shr_lin_relu_kernel(
                     if i in SCALAR_PLANES:
                         halves = dst.bitcast(BF16).rearrange("p (s j) -> p j s", j=2)
                         for j in (1, 0):
-                            window = singles[:, single_start[i] + j * T : single_start[i] + (j + 2) * T]
+                            window = singles[:, single_start[i] + j * T : single_start[i] + j * T + WINDOW]
                             nc.scalar.activation(halves[:, j, :], window.indirect(tokens), ACT.Copy)
                     else:
                         window = pairs[:, plane_start(i) : plane_start(i) + WINDOW]
                         nc.vector.tensor_copy(dst, window.indirect(tokens))
             gathered[number] = picked
             places[number] = place
+
+        def weave(number, words):
+            passes, s0, n = chunks[number]
+            picked = gathered[number]
+            width = n * len(passes)
+            if number == GPSIMD_WEAVES:
+                gpsimd_copy(
+                    words[:, :width].bitcast(BF16).rearrange("p (s u j) -> p s u j", u=2, j=2),
+                    picked[:, :width].bitcast(BF16).rearrange("p (u s j) -> p s u j", u=2, j=2),
+                )
+            if number == VECTOR_WEAVES:
+                nc.vector.tensor_copy(
+                    words[:, :width].bitcast(I32).rearrange("p (s u) -> p s u", u=2),
+                    picked[:, :width].bitcast(I32).rearrange("p (u s) -> p s u", u=2),
+                )
+            if number in (GPSIMD_WEAVES, VECTOR_WEAVES):
+                nc.scalar.copy(
+                    words[:, width:].rearrange("p (s u) -> p s u", u=2),
+                    picked[:, width:].rearrange("p (u s) -> p s u", u=2),
+                )
+            else:
+                nc.scalar.copy(
+                    words[:].rearrange("p (m s u) -> p m s u", m=len(passes), u=2),
+                    picked[:].rearrange("p (m u s) -> p m s u", m=len(passes), u=2),
+                )
 
         def finish(number):
             passes, s0, n = chunks[number]
@@ -176,42 +210,24 @@ def tile_moe_shr_lin_relu_kernel(
                     e = first // C
                     acc = banks.tile([P, width], F32, name="acc")
                     for slot in range(first, first + width, GROUP):
-                        for a2 in range(PASSES):
-                            multiply(acc[:, slot - first : slot - first + GROUP], e, a2, *made[(a2, slot)])
+                        for a in range(PASSES):
+                            multiply(acc[:, slot - first : slot - first + GROUP], e, a, *made[(a, slot)])
                     nc.scalar.activation(y[:, first : first + width], acc[:], ACT.Relu, bias=bias[:, e : e + 1])
 
-        for number in range(AHEAD):
-            gather(number, number)
         half = len(chunks) // 2
         order = [0]
         for j in range(half - 1):
             order.extend([j + 1, half + j])
         order.append(len(chunks) - 1)
+
+        for number in range(AHEAD):
+            gather(number, number)
         for step, number in enumerate(order):
             passes, s0, n = chunks[number]
             width = n * len(passes)
             tag = f"early{step}" if step < PASSES - 1 else f"stage{step % STAGES}"
             words = keep.tile([P, 2 * width], U32, name="words", tag=tag, align_bytes=64)
-            if number in (GPSIMD_WEAVES, VECTOR_WEAVES):
-                if number == GPSIMD_WEAVES:
-                    gpsimd_cast(
-                        words[:, :width].bitcast(BF16).rearrange("p (s u j) -> p s u j", u=2, j=2),
-                        gathered[number][:, :width].bitcast(BF16).rearrange("p (u s j) -> p s u j", u=2, j=2),
-                    )
-                else:
-                    nc.vector.tensor_copy(
-                        words[:, :width].bitcast(I32).rearrange("p (s u) -> p s u", u=2),
-                        gathered[number][:, :width].bitcast(I32).rearrange("p (u s) -> p s u", u=2),
-                    )
-                nc.scalar.copy(
-                    words[:, width:].rearrange("p (s u) -> p s u", u=2),
-                    gathered[number][:, width:].rearrange("p (u s) -> p s u", u=2),
-                )
-            else:
-                nc.scalar.copy(
-                    words[:].rearrange("p (m s u) -> p m s u", m=len(passes), u=2),
-                    gathered[number][:].rearrange("p (m u s) -> p m s u", m=len(passes), u=2),
-                )
+            weave(number, words)
             codes = keep.tile([P, width], U32, name=f"codes{number}", align_bytes=64)
             scales = keep.tile([P, width], U8, name=f"scales{number}", align_bytes=64)
             nc.vector.quantize_mx(out=codes[:].bitcast(FP8X4), scales=scales[:], in_=words[:].bitcast(BF16))
@@ -220,7 +236,7 @@ def tile_moe_shr_lin_relu_kernel(
                     cols = slice(m * n + slot - s0, m * n + slot - s0 + GROUP)
                     made[(a, slot)] = (codes[:, cols], scales[:, cols])
             if step < PASSES - 1:
-                cast_shared(step, tag)
+                round_shared(step, tag)
             if step + AHEAD < len(chunks):
                 gather(step + AHEAD, places[number])
             if step >= LAG:
@@ -228,58 +244,58 @@ def tile_moe_shr_lin_relu_kernel(
         for number in order[-LAG:]:
             finish(number)
 
-        acc = shared_bank.tile([P, T], F32, name="shared_acc")
+        shared_acc = shared_bank.tile([P, T], F32, name="shared_acc")
         last = len(chunks) - 1
         codes_first = keep.tile([P, T], U32, name="codes_first", tag=f"picked{places[last - 1]}", align_bytes=64)
         codes_rest = keep.tile([P, (PASSES - 1) * T], U32, name="codes_rest", tag=f"picked{places[last]}", align_bytes=64)
         for a in range(PASSES):
-            codes = codes_first[:] if a == 0 else codes_rest[:, (a - 1) * T : a * T]
-            scales = keep.tile([P, T], U8, name=f"shared_scales{a}", align_bytes=64)
+            shared_codes = codes_first[:] if a == 0 else codes_rest[:, (a - 1) * T : a * T]
+            shared_scales = keep.tile([P, T], U8, name=f"shared_scales{a}", align_bytes=64)
             nc.vector.quantize_mx(
-                out=codes.bitcast(FP8X4),
-                scales=scales[:],
-                in_=shared_words[a][:].rearrange("p t j -> p (t j)"),
+                out=shared_codes.bitcast(FP8X4),
+                scales=shared_scales[:],
+                in_=shared_words[a][:].rearrange("p t d -> p (t d)"),
             )
-            multiply(acc[:], E, a, codes, scales[:])
-        nc.scalar.activation(ys[:], acc[:], ACT.Relu, bias=bias[:, E : E + 1])
-
-        def add_turned(acc, src, first, last):
-            nc.tensor.matmul(acc, lhsT=src, rhs=identity[:], start=first, stop=last, is_transpose=True)
-
-        def turn(src):
-            bank = banks.tile([P, BLOCKS, P], F32, name="bank", tag="acc")
-            for k in range(BLOCKS):
-                nc.tensor.transpose(bank[:, k, :], src[:, k * P : (k + 1) * P], identity[:])
-            return bank
+            multiply(shared_acc[:], E, a, shared_codes, shared_scales[:])
+        nc.scalar.activation(ys[:], shared_acc[:], ACT.Relu, bias=bias[:, E : E + 1])
 
         picked_y = keep.tile([P, TOP, TURNED], F32, name="picked_y")
         for r in range(TOP):
-            nc.vector.tensor_copy(picked_y[:, r, :], y[:].indirect(token_slots[r][:, : TURNED // 16]))
-        terms = keep.tile([P, TOP + 1, BLOCKS, P], F32, name="terms")
+            nc.vector.tensor_copy(picked_y[:, r, :], y[:].indirect(token_slots[r][:, : TURNED // PER_COLUMN]))
+        terms = keep.tile([P, TOP, BLOCKS, P], F32, name="terms")
         sums = []
         for k in range(BLOCKS):
             sums.append(banks.tile([P, P], F32, name="total", tag="acc"))
         for r in range(TOP):
-            bank = turn(picked_y[:, r, :])
+            turned = banks.tile([P, BLOCKS, P], F32, name="turned", tag="acc")
             for k in range(BLOCKS):
-                nc.scalar.activation(terms[:, r, k, :], bank[:, k, :], ACT.Copy, scale=token_gates[r][:, k : k + 1])
-                add_turned(sums[k][:], terms[:, r, k, :], r == 0, r == TOP - 1)
-            if r == 0:
-                nc.scalar.copy(terms[:, TOP, :, :], turn(ys[:])[:])
-                for k in range(BLOCKS):
-                    add_turned(sums[k][:], terms[:, TOP, k, :], False, False)
-        result = keep.tile([P, TURNED], F32, name="result")
-        for k in range(BLOCKS):
-            nc.scalar.copy(result[:, k * P : (k + 1) * P], sums[k][:])
-        nc.sync.dma_start(out[:, :TURNED], result[:])
+                nc.tensor.transpose(turned[:, k, :], picked_y[:, r, k * P : (k + 1) * P], identity[:])
+            for k in range(BLOCKS):
+                nc.scalar.activation(terms[:, r, k, :], turned[:, k, :], ACT.Copy, scale=token_gates[r][:, k : k + 1])
+                nc.tensor.matmul(
+                    sums[k][:],
+                    lhsT=terms[:, r, k, :],
+                    rhs=identity[:],
+                    start=(r == 0),
+                    stop=(r == TOP - 1),
+                    is_transpose=True,
+                )
 
         z = keep.tile([P, TOP, T - TURNED], F32, name="z")
         rest = keep.tile([P, T - TURNED], F32, name="rest")
         for r in range(TOP + 1):
             if r < TOP:
-                nc.vector.tensor_tensor(z[:, r, :], y[:].indirect(token_slots[r][:, TURNED // 16 :]), gates[:, r, :], ALU.mult)
+                slots_of_rest = token_slots[r][:, TURNED // PER_COLUMN :]
+                nc.vector.tensor_tensor(z[:, r, :], y[:].indirect(slots_of_rest), gates[:, r, :], ALU.mult)
             if r == 1:
                 nc.vector.tensor_tensor(rest[:], ys[:, TURNED:], z[:, 0, :], ALU.add)
             elif r > 1:
                 nc.vector.tensor_tensor(rest[:], rest[:], z[:, r - 1, :], ALU.add)
         nc.sync.dma_start(out[:, TURNED:], rest[:])
+
+        result = keep.tile([P, TURNED], F32, name="result")
+        for k in range(BLOCKS):
+            cols = slice(k * P, (k + 1) * P)
+            nc.vector.tensor_tensor(result[:, cols], sums[k][:], ys[:, cols], ALU.add)
+        nc.sync.dma_start(out[:, : TURNED - P], result[:, : TURNED - P])
+        nc.scalar.dma_start(out[:, TURNED - P : TURNED], result[:, TURNED - P :])

from contextlib import ExitStack

import concourse.mybir as mybir
from concourse.masks import make_identity

K, T, E, C, N = 2048, 512, 8, 256, 128
TOP = 4
SLOTS = E * C
FLOPS = 2 * K * N * (SLOTS + T)

F32 = mybir.dt.float32
BF16 = mybir.dt.bfloat16
I32 = mybir.dt.int32
U32 = mybir.dt.uint32
U16 = mybir.dt.uint16
U8 = mybir.dt.uint8
FP8X4 = mybir.dt.float8_e4m3fn_x4
FP4X4 = mybir.dt.float4_e2m1fn_x4
ACT = mybir.ActivationFunctionType
ALU = mybir.AluOpType

P = 128
PASSES = K // (4 * P)
PLANES = 2 * PASSES
PER_COLUMN = 16
GROUP = 128
HALF = T // 2

SPARE = 2 * T
WINDOW = T + SPARE

CHUNK = 512
AHEAD = 4
STAGES = 3
LAG = 2
BANKS = 7

SCALAR_PLANES = (1, PLANES - 1)
GPSIMD_WEAVES = 6
VECTOR_WEAVES = 4

BLOCKS = 3
TURNED = BLOCKS * P


def tile_moe_shr_lin_relu_kernel(
    tc, xT, w_words, w_scales, b, gate, offs, pos1, pos2, pos3, pos4, out
):
    nc = tc.nc
    with ExitStack() as ctx:
        keep = ctx.enter_context(tc.tile_pool(name="keep", bufs=1))
        banks = ctx.enter_context(tc.psum_pool(name="banks", bufs=BANKS))
        shared_bank = ctx.enter_context(tc.psum_pool(name="shared_bank", bufs=1))

        x_rows = xT.rearrange("(a p u j) t -> a u p j t", a=PASSES, p=P, u=2, j=2)
        slot_tokens = keep.tile([P, SLOTS // PER_COLUMN], U16, name="slot_tokens")
        raw = []
        for a in range(PASSES):
            raw.append(keep.tile([P, 4 * T], F32, name=f"raw{a}"))

        def raw_plane(i):
            u = 1 - i % 2
            return raw[i // 2][:, 2 * u * T : 2 * (u + 1) * T].rearrange("p (j t) -> p j t", j=2)

        for h in range(2):
            cols = slice(h * HALF, (h + 1) * HALF)
            nc.sync.dma_start(raw_plane(0)[:, :, cols], x_rows[0, 1][:, :, cols])
        nc.sync.dma_start(slot_tokens[:], offs)
        for j in (1, 0):
            nc.sync.dma_start(raw_plane(1)[:, j, :], x_rows[0, 0][:, j, :])
        for i in range(2, PLANES):
            nc.sync.dma_start(raw_plane(i), x_rows[i // 2, 1 - i % 2])

        paired = [i for i in range(PLANES) if i not in SCALAR_PLANES]
        pairs = keep.tile([P, len(paired) * T + SPARE], U32, name="pairs", align_bytes=64)
        nc.vector.memset(pairs[:, len(paired) * T :], 0)
        singles = keep.tile([P, 2 * len(SCALAR_PLANES) * T + SPARE], BF16, name="singles", align_bytes=64)
        nc.vector.memset(singles[:, 2 * len(SCALAR_PLANES) * T :], 0.0)

        w_scale = keep.tile([P, (E + 1) * PASSES, N], U8, name="w_scale", align_bytes=64)
        nc.gpsimd.memset(w_scale[:].bitcast(I32), 0)
        w_code = keep.tile([P, (E + 1) * PASSES, 2 * N], U8, name="w_code", align_bytes=64)
        nc.sync.dma_start(w_code[:].bitcast(I32), w_words.rearrange("e a p c -> p (e a) c").bitcast(I32))
        scale_rows = w_scales.rearrange("e a (q r) n -> r q (e a) n", r=4)
        for r in range(4):
            nc.sync.dma_start(w_scale[r:P:32, :, :].bitcast(I32), scale_rows[r].bitcast(I32))

        bias = keep.tile([P, E + 1], F32, name="bias")
        nc.sync.dma_start(bias[:], b)
        gates = keep.tile([P, TOP, T - TURNED], F32, name="gates")
        nc.sync.dma_start(gates[:], gate.rearrange("r p t -> p r t")[:, :, TURNED:])
        token_gates = []
        for r in range(TOP):
            column = keep.tile([P, BLOCKS], F32, name=f"token_gates{r}")
            with nc.allow_non_contiguous_dma(reason="one gate value a partition"):
                nc.sync.dma_start(column[:], gate[r, 0, :TURNED].rearrange("(k p) -> p k", p=P))
            token_gates.append(column)
        identity = keep.tile([P, P], F32, name="identity")
        make_identity(nc, identity[:])
        token_slots = []
        for r, pos in enumerate((pos1, pos2, pos3, pos4)):
            inverse = keep.tile([P, T // PER_COLUMN], U16, name=f"token_slots{r}")
            nc.sync.dma_start(inverse[:], pos)
            token_slots.append(inverse)

        def plane_start(i):
            return (len(paired) - 1 - paired.index(i)) * T

        def pair_view(i):
            return pairs[:, plane_start(i) : plane_start(i) + T].bitcast(BF16).rearrange("p (t j) -> p t j", j=2)

        def gpsimd_copy(dst, src):
            nc.gpsimd.tensor_scalar(dst, src, 1.0, 0.0, ALU.mult, ALU.add)

        for h in range(2):
            cols = slice(h * HALF, (h + 1) * HALF)
            nc.vector.tensor_copy(pair_view(0)[:, cols, :], raw_plane(0).rearrange("p j t -> p t j")[:, cols, :])

        single_start = {i: 2 * T * (len(SCALAR_PLANES) - 1 - m) for m, i in enumerate(SCALAR_PLANES)}

        def single_rows(i):
            return singles[:, single_start[i] : single_start[i] + 2 * T], raw_plane(i).rearrange("p j t -> p (j t)")

        rounded_rows, raw_rows = single_rows(SCALAR_PLANES[0])
        nc.scalar.activation(rounded_rows[:, T:], raw_rows[:, T:], ACT.Copy)
        gpsimd_copy(rounded_rows[:, :T], raw_rows[:, :T])
        for i in paired[1:]:
            gpsimd_copy(pair_view(i), raw_plane(i).rearrange("p j t -> p t j"))
        gpsimd_copy(*single_rows(SCALAR_PLANES[1]))

        shared_words = {}

        def round_shared(a, tag):
            tokens_of_pass = keep.tile([P, T, 4], BF16, name=f"shared_words{a}", tag=tag, align_bytes=64)
            gpsimd_copy(tokens_of_pass[:], raw[a][:].rearrange("p (d t) -> p t d", d=4))
            shared_words[a] = tokens_of_pass

        round_shared(PASSES - 1, "shared_words")

        y = keep.tile([P, SLOTS], F32, name="y")
        ys = keep.tile([P, T], F32, name="ys")

        chunks = [((a,), s0, 2 * CHUNK) for s0 in range(0, SLOTS, 2 * CHUNK) for a in (0, 1)]
        chunks.extend([((2, 3), s0, CHUNK) for s0 in range(0, SLOTS, CHUNK)])

        made = {}
        gathered = {}
        places = {}

        def multiply(acc, e, a, codes, scales):
            nc.tensor.matmul_mx(
                out=acc,
                lhsT=w_code[:, e * PASSES + a, :].bitcast(FP4X4),
                lhsT_scale=w_scale[:, e * PASSES + a, :],
                rhs=codes.bitcast(FP8X4),
                rhs_scale=scales,
                start=(a == 0),
                stop=(a == PASSES - 1),
            )

        def gather(number, place):
            passes, s0, n = chunks[number]
            picked = keep.tile([P, 2 * n * len(passes)], U32, name="picked", tag=f"picked{place}", align_bytes=64)
            tokens = slot_tokens[:, s0 // PER_COLUMN : (s0 + n) // PER_COLUMN]
            for m, a in enumerate(passes):
                for v in range(2):
                    i = 2 * a + v
                    dst = picked[:, (2 * m + 1 - v) * n : (2 * m + 2 - v) * n]
                    if i in SCALAR_PLANES:
                        halves = dst.bitcast(BF16).rearrange("p (s j) -> p j s", j=2)
                        for j in (1, 0):
                            window = singles[:, single_start[i] + j * T : single_start[i] + j * T + WINDOW]
                            nc.scalar.activation(halves[:, j, :], window.indirect(tokens), ACT.Copy)
                    else:
                        window = pairs[:, plane_start(i) : plane_start(i) + WINDOW]
                        nc.vector.tensor_copy(dst, window.indirect(tokens))
            gathered[number] = picked
            places[number] = place

        def weave(number, words):
            passes, s0, n = chunks[number]
            picked = gathered[number]
            width = n * len(passes)
            if number == GPSIMD_WEAVES:
                gpsimd_copy(
                    words[:, :width].bitcast(BF16).rearrange("p (s u j) -> p s u j", u=2, j=2),
                    picked[:, :width].bitcast(BF16).rearrange("p (u s j) -> p s u j", u=2, j=2),
                )
            if number == VECTOR_WEAVES:
                nc.vector.tensor_copy(
                    words[:, :width].bitcast(I32).rearrange("p (s u) -> p s u", u=2),
                    picked[:, :width].bitcast(I32).rearrange("p (u s) -> p s u", u=2),
                )
            if number in (GPSIMD_WEAVES, VECTOR_WEAVES):
                nc.scalar.copy(
                    words[:, width:].rearrange("p (s u) -> p s u", u=2),
                    picked[:, width:].rearrange("p (u s) -> p s u", u=2),
                )
            else:
                nc.scalar.copy(
                    words[:].rearrange("p (m s u) -> p m s u", m=len(passes), u=2),
                    picked[:].rearrange("p (m u s) -> p m s u", m=len(passes), u=2),
                )

        def finish(number):
            passes, s0, n = chunks[number]
            if PASSES - 1 in passes:
                width = GROUP if number >= len(chunks) - 2 else C
                for first in range(s0, s0 + n, width):
                    e = first // C
                    acc = banks.tile([P, width], F32, name="acc")
                    for slot in range(first, first + width, GROUP):
                        for a in range(PASSES):
                            multiply(acc[:, slot - first : slot - first + GROUP], e, a, *made[(a, slot)])
                    nc.scalar.activation(y[:, first : first + width], acc[:], ACT.Relu, bias=bias[:, e : e + 1])

        half = len(chunks) // 2
        order = [0]
        for j in range(half - 1):
            order.extend([j + 1, half + j])
        order.append(len(chunks) - 1)

        for number in range(AHEAD):
            gather(number, number)
        for step, number in enumerate(order):
            passes, s0, n = chunks[number]
            width = n * len(passes)
            tag = f"early{step}" if step < PASSES - 1 else f"stage{step % STAGES}"
            words = keep.tile([P, 2 * width], U32, name="words", tag=tag, align_bytes=64)
            weave(number, words)
            codes = keep.tile([P, width], U32, name=f"codes{number}", align_bytes=64)
            scales = keep.tile([P, width], U8, name=f"scales{number}", align_bytes=64)
            nc.vector.quantize_mx(out=codes[:].bitcast(FP8X4), scales=scales[:], in_=words[:].bitcast(BF16))
            for m, a in enumerate(passes):
                for slot in range(s0, s0 + n, GROUP):
                    cols = slice(m * n + slot - s0, m * n + slot - s0 + GROUP)
                    made[(a, slot)] = (codes[:, cols], scales[:, cols])
            if step < PASSES - 1:
                round_shared(step, tag)
            if step + AHEAD < len(chunks):
                gather(step + AHEAD, places[number])
            if step >= LAG:
                finish(order[step - LAG])
        for number in order[-LAG:]:
            finish(number)

        shared_acc = shared_bank.tile([P, T], F32, name="shared_acc")
        last = len(chunks) - 1
        codes_first = keep.tile([P, T], U32, name="codes_first", tag=f"picked{places[last - 1]}", align_bytes=64)
        codes_rest = keep.tile([P, (PASSES - 1) * T], U32, name="codes_rest", tag=f"picked{places[last]}", align_bytes=64)
        for a in range(PASSES):
            shared_codes = codes_first[:] if a == 0 else codes_rest[:, (a - 1) * T : a * T]
            shared_scales = keep.tile([P, T], U8, name=f"shared_scales{a}", align_bytes=64)
            nc.vector.quantize_mx(
                out=shared_codes.bitcast(FP8X4),
                scales=shared_scales[:],
                in_=shared_words[a][:].rearrange("p t d -> p (t d)"),
            )
            multiply(shared_acc[:], E, a, shared_codes, shared_scales[:])
        nc.scalar.activation(ys[:], shared_acc[:], ACT.Relu, bias=bias[:, E : E + 1])

        picked_y = keep.tile([P, TOP, TURNED], F32, name="picked_y")
        for r in range(TOP):
            nc.vector.tensor_copy(picked_y[:, r, :], y[:].indirect(token_slots[r][:, : TURNED // PER_COLUMN]))
        terms = keep.tile([P, TOP, BLOCKS, P], F32, name="terms")
        sums = []
        for k in range(BLOCKS):
            sums.append(banks.tile([P, P], F32, name="total", tag="acc"))
        for r in range(TOP):
            turned = banks.tile([P, BLOCKS, P], F32, name="turned", tag="acc")
            for k in range(BLOCKS):
                nc.tensor.transpose(turned[:, k, :], picked_y[:, r, k * P : (k + 1) * P], identity[:])
            for k in range(BLOCKS):
                nc.scalar.activation(terms[:, r, k, :], turned[:, k, :], ACT.Copy, scale=token_gates[r][:, k : k + 1])
                nc.tensor.matmul(
                    sums[k][:],
                    lhsT=terms[:, r, k, :],
                    rhs=identity[:],
                    start=(r == 0),
                    stop=(r == TOP - 1),
                    is_transpose=True,
                )

        z = keep.tile([P, TOP, T - TURNED], F32, name="z")
        rest = keep.tile([P, T - TURNED], F32, name="rest")
        for r in range(TOP + 1):
            if r < TOP:
                slots_of_rest = token_slots[r][:, TURNED // PER_COLUMN :]
                nc.vector.tensor_tensor(z[:, r, :], y[:].indirect(slots_of_rest), gates[:, r, :], ALU.mult)
            if r == 1:
                nc.vector.tensor_tensor(rest[:], ys[:, TURNED:], z[:, 0, :], ALU.add)
            elif r > 1:
                nc.vector.tensor_tensor(rest[:], rest[:], z[:, r - 1, :], ALU.add)
        nc.sync.dma_start(out[:, TURNED:], rest[:])

        result = keep.tile([P, TURNED], F32, name="result")
        for k in range(BLOCKS):
            cols = slice(k * P, (k + 1) * P)
            nc.vector.tensor_tensor(result[:, cols], sums[k][:], ys[:, cols], ALU.add)
        nc.sync.dma_start(out[:, : TURNED - P], result[:, : TURNED - P])
        nc.scalar.dma_start(out[:, TURNED - P : TURNED], result[:, TURNED - P :])
